import numpy as np
import ml_dtypes

BF16 = ml_dtypes.bfloat16


def bf(x):
    return np.asarray(x, np.float32).astype(BF16)


def f32(x):
    return np.asarray(x, np.float32)


def f64(x):
    return np.asarray(x).astype(np.float64)


def striped(idx):
    return np.tile(idx.reshape(-1, 16).T, (8, 1))


S, K, M, N = 2048, 256, 256, 2048


def setup_inputs():
    return {"table": bf(np.random.standard_normal((S, K))), "w": bf(np.random.standard_normal((K, M)) / np.sqrt(K)), "b": f32(0.5 * np.random.standard_normal((M, 1))), "offs": striped(np.random.permutation(S))}


def reference(table, w, b, offs):
    idx = offs[:16].T.reshape(-1)
    x = f64(table)[idx].T
    y = f64(w).T @ x
    return np.maximum(y + f64(b), 0.0)

@@ -1,0 +1,82 @@
+import concourse.mybir as mybir
+from concourse.masks import make_identity
+
+P = 128
+S, K, M, N = 2048, 256, 256, 2048
+PIECE = 512
+K_BLOCKS = K // P
+M_BLOCKS = M // P
+PIECES = N // PIECE
+ROW_BLOCKS = S // P
+LOADS = 4
+BLOCKS_A_LOAD = ROW_BLOCKS // LOADS
+
+FLOPS = 2 * K * M * N
+
+BF16, F32, U16 = mybir.dt.bfloat16, mybir.dt.float32, mybir.dt.uint16
+ADD, MAX = mybir.AluOpType.add, mybir.AluOpType.max
+RELU = mybir.ActivationFunctionType.Relu
+
+
+def tile_gather_matmul_kernel(tc, table, w, b, offs, out):
+    nc = tc.nc
+    with (
+        tc.tile_pool(name="held", bufs=1) as held,
+        tc.tile_pool(name="staging", bufs=4) as staging,
+        tc.psum_pool(name="flip", bufs=2) as flip,
+        tc.psum_pool(name="sums", bufs=6) as sums,
+    ):
+        offsets = held.tile([P, N // 16], U16, name="offsets")
+        nc.sync.dma_start(offsets[:], offs)
+
+        table_rows = table.rearrange("(a p) k -> p a k", p=P)
+        queues = [nc.sync, nc.scalar]
+        tokens = []
+        for c in range(LOADS):
+            rows = held.tile([P, BLOCKS_A_LOAD, K], BF16, name="rows%d" % c)
+            queues[c % 2].dma_start(rows[:], table_rows[:, c * BLOCKS_A_LOAD : (c + 1) * BLOCKS_A_LOAD, :])
+            tokens.append(rows)
+
+        weights = held.tile([P, K_BLOCKS, M], BF16, name="weights")
+        nc.gpsimd.dma_start(weights[:], w.rearrange("(kb p) m -> p kb m", p=P))
+        bias = held.tile([P, M_BLOCKS], F32, name="bias")
+        nc.gpsimd.dma_start(bias[:], b.rearrange("(mb p) o -> p (mb o)", p=P))
+
+        identity = held.tile([P, P], BF16, name="identity")
+        make_identity(nc, identity[:])
+
+        windows = [held.tile([P, S], BF16, name="window%d" % kb) for kb in range(K_BLOCKS)]
+        width = BLOCKS_A_LOAD * P
+        for c in range(LOADS):
+            for kb in range(K_BLOCKS):
+                flipped = flip.tile([P, width], BF16, name="flipped")
+                for a in range(BLOCKS_A_LOAD):
+                    nc.tensor.transpose(
+                        flipped[:, a * P : (a + 1) * P],
+                        tokens[c][:, a, kb * P : (kb + 1) * P],
+                        identity[:],
+                    )
+                target = windows[kb][:, c * width : (c + 1) * width]
+                if kb == 0:
+                    nc.vector.tensor_copy(target, flipped[:])
+                else:
+                    nc.scalar.copy(target, flipped[:])
+
+        for piece in range(PIECES):
+            picked = offsets[:, piece * (PIECE // 16) : (piece + 1) * (PIECE // 16)]
+            for mb in range(M_BLOCKS):
+                bank = sums.tile([P, PIECE], F32, name="bank")
+                for kb in range(K_BLOCKS):
+                    nc.tensor.matmul(
+                        bank[:],
+                        weights[:, kb, mb * P : (mb + 1) * P],
+                        windows[kb][:].indirect(picked),
+                        start=(kb == 0),
+                        stop=(kb == K_BLOCKS - 1),
+                    )
+                result = staging.tile([P, PIECE], F32, name="result")
+                if mb == 0:
+                    nc.vector.tensor_scalar(result[:], bank[:], bias[:, mb : mb + 1], 0.0, op0=ADD, op1=MAX)
+                else:
+                    nc.scalar.activation(result[:], bank[:], RELU, bias=bias[:, mb : mb + 1])
+                nc.sync.dma_start(out[mb * P : (mb + 1) * P, piece * PIECE : (piece + 1) * PIECE], result[:])

@@ -23,60 +23,58 @@ def tile_gather_matmul_kernel(tc, table, w, b, offs, out):
     with (
         tc.tile_pool(name="held", bufs=1) as held,
         tc.tile_pool(name="staging", bufs=4) as staging,
-        tc.psum_pool(name="flip", bufs=2) as flip,
-        tc.psum_pool(name="sums", bufs=6) as sums,
     ):
-        offsets = held.tile([P, N // 16], U16, name="offsets")
-        nc.sync.dma_start(offsets[:], offs)
-
-        table_rows = table.rearrange("(a p) k -> p a k", p=P)
-        queues = [nc.sync, nc.scalar]
-        tokens = []
-        for c in range(LOADS):
-            rows = held.tile([P, BLOCKS_A_LOAD, K], BF16, name="rows%d" % c)
-            queues[c % 2].dma_start(rows[:], table_rows[:, c * BLOCKS_A_LOAD : (c + 1) * BLOCKS_A_LOAD, :])
-            tokens.append(rows)
-
-        weights = held.tile([P, K_BLOCKS, M], BF16, name="weights")
-        nc.gpsimd.dma_start(weights[:], w.rearrange("(kb p) m -> p kb m", p=P))
-        bias = held.tile([P, M_BLOCKS], F32, name="bias")
-        nc.gpsimd.dma_start(bias[:], b.rearrange("(mb p) o -> p (mb o)", p=P))
-
         identity = held.tile([P, P], BF16, name="identity")
         make_identity(nc, identity[:])
 
+        table_rows = table.rearrange("(a p) k -> p a k", p=P)
+        tokens = []
+        for c in range(LOADS):
+            rows = held.tile([P, BLOCKS_A_LOAD, K], BF16, name="rows%d" % c)
+            nc.sync.dma_start(rows[:], table_rows[:, c * BLOCKS_A_LOAD : (c + 1) * BLOCKS_A_LOAD, :])
+            tokens.append(rows)
+
+        offsets = held.tile([P, N // 16], U16, name="offsets")
+        nc.sync.dma_start(offsets[:], offs)
+        weights = held.tile([P, K_BLOCKS, M], BF16, name="weights")
+        nc.scalar.dma_start(weights[:], w.rearrange("(kb p) m -> p kb m", p=P))
+        bias = held.tile([P, M_BLOCKS], F32, name="bias")
+        nc.scalar.dma_start(bias[:], b.rearrange("(mb p) o -> p (mb o)", p=P))
+
         windows = [held.tile([P, S], BF16, name="window%d" % kb) for kb in range(K_BLOCKS)]
         width = BLOCKS_A_LOAD * P
-        for c in range(LOADS):
-            for kb in range(K_BLOCKS):
-                flipped = flip.tile([P, width], BF16, name="flipped")
-                for a in range(BLOCKS_A_LOAD):
-                    nc.tensor.transpose(
-                        flipped[:, a * P : (a + 1) * P],
-                        tokens[c][:, a, kb * P : (kb + 1) * P],
-                        identity[:],
-                    )
-                target = windows[kb][:, c * width : (c + 1) * width]
-                if kb == 0:
-                    nc.vector.tensor_copy(target, flipped[:])
-                else:
-                    nc.scalar.copy(target, flipped[:])
-
-        for piece in range(PIECES):
-            picked = offsets[:, piece * (PIECE // 16) : (piece + 1) * (PIECE // 16)]
-            for mb in range(M_BLOCKS):
-                bank = sums.tile([P, PIECE], F32, name="bank")
+        with tc.psum_pool(name="flip", bufs=LOADS * K_BLOCKS) as flip:
+            for c in range(LOADS):
                 for kb in range(K_BLOCKS):
-                    nc.tensor.matmul(
-                        bank[:],
-                        weights[:, kb, mb * P : (mb + 1) * P],
-                        windows[kb][:].indirect(picked),
-                        start=(kb == 0),
-                        stop=(kb == K_BLOCKS - 1),
-                    )
-                result = staging.tile([P, PIECE], F32, name="result")
-                if mb == 0:
-                    nc.vector.tensor_scalar(result[:], bank[:], bias[:, mb : mb + 1], 0.0, op0=ADD, op1=MAX)
-                else:
-                    nc.scalar.activation(result[:], bank[:], RELU, bias=bias[:, mb : mb + 1])
-                nc.sync.dma_start(out[mb * P : (mb + 1) * P, piece * PIECE : (piece + 1) * PIECE], result[:])
+                    flipped = flip.tile([P, width], BF16, name="flipped")
+                    for a in range(BLOCKS_A_LOAD):
+                        nc.tensor.transpose(
+                            flipped[:, a * P : (a + 1) * P],
+                            tokens[c][:, a, kb * P : (kb + 1) * P],
+                            identity[:],
+                        )
+                    target = windows[kb][:, c * width : (c + 1) * width]
+                    if kb == 0:
+                        nc.vector.tensor_copy(target, flipped[:])
+                    else:
+                        nc.scalar.copy(target, flipped[:])
+
+        with tc.psum_pool(name="sums", bufs=PIECES * M_BLOCKS) as sums:
+            for piece in range(PIECES):
+                picked = offsets[:, piece * (PIECE // 16) : (piece + 1) * (PIECE // 16)]
+                for mb in range(M_BLOCKS):
+                    bank = sums.tile([P, PIECE], F32, name="bank")
+                    for kb in range(K_BLOCKS):
+                        nc.tensor.matmul(
+                            bank[:],
+                            weights[:, kb, mb * P : (mb + 1) * P],
+                            windows[kb][:].indirect(picked),
+                            start=(kb == 0),
+                            stop=(kb == K_BLOCKS - 1),
+                        )
+                    result = staging.tile([P, PIECE], F32, name="result")
+                    if mb == 0:
+                        nc.vector.tensor_scalar(result[:], bank[:], bias[:, mb : mb + 1], 0.0, op0=ADD, op1=MAX)
+                    else:
+                        nc.scalar.activation(result[:], bank[:], RELU, bias=bias[:, mb : mb + 1])
+                    nc.sync.dma_start(out[mb * P : (mb + 1) * P, piece * PIECE : (piece + 1) * PIECE], result[:])

@@ -4,12 +4,12 @@ from concourse.masks import make_identity
 P = 128
 S, K, M, N = 2048, 256, 256, 2048
 PIECE = 512
-K_BLOCKS = K // P
+HALVES = K // P
 M_BLOCKS = M // P
 PIECES = N // PIECE
-ROW_BLOCKS = S // P
 LOADS = 4
-BLOCKS_A_LOAD = ROW_BLOCKS // LOADS
+TOKENS_A_LOAD = S // LOADS
+NEIGHBOURS = TOKENS_A_LOAD // P
 
 FLOPS = 2 * K * M * N
 
@@ -23,58 +23,52 @@ def tile_gather_matmul_kernel(tc, table, w, b, offs, out):
     with (
         tc.tile_pool(name="held", bufs=1) as held,
         tc.tile_pool(name="staging", bufs=4) as staging,
+        tc.psum_pool(name="flip", bufs=LOADS) as flip,
+        tc.psum_pool(name="sums", bufs=2) as sums,
     ):
-        identity = held.tile([P, P], BF16, name="identity")
+        identity = held.tile([P, P], F32, name="identity")
         make_identity(nc, identity[:])
 
-        table_rows = table.rearrange("(a p) k -> p a k", p=P)
+        table_rows = table.rearrange("(c p a) k -> c p a k", p=P, a=NEIGHBOURS)
         tokens = []
         for c in range(LOADS):
-            rows = held.tile([P, BLOCKS_A_LOAD, K], BF16, name="rows%d" % c)
-            nc.sync.dma_start(rows[:], table_rows[:, c * BLOCKS_A_LOAD : (c + 1) * BLOCKS_A_LOAD, :])
+            rows = held.tile([P, NEIGHBOURS, K], BF16, name="rows%d" % c)
+            nc.sync.dma_start(rows[:], table_rows[c])
             tokens.append(rows)
 
         offsets = held.tile([P, N // 16], U16, name="offsets")
         nc.sync.dma_start(offsets[:], offs)
-        weights = held.tile([P, K_BLOCKS, M], BF16, name="weights")
-        nc.scalar.dma_start(weights[:], w.rearrange("(kb p) m -> p kb m", p=P))
+        weights = held.tile([P, HALVES, M], BF16, name="weights")
+        nc.scalar.dma_start(weights[:], w.rearrange("(p h) m -> p h m", h=HALVES))
         bias = held.tile([P, M_BLOCKS], F32, name="bias")
         nc.scalar.dma_start(bias[:], b.rearrange("(mb p) o -> p (mb o)", p=P))
 
-        windows = [held.tile([P, S], BF16, name="window%d" % kb) for kb in range(K_BLOCKS)]
-        width = BLOCKS_A_LOAD * P
-        with tc.psum_pool(name="flip", bufs=LOADS * K_BLOCKS) as flip:
-            for c in range(LOADS):
-                for kb in range(K_BLOCKS):
-                    flipped = flip.tile([P, width], BF16, name="flipped")
-                    for a in range(BLOCKS_A_LOAD):
-                        nc.tensor.transpose(
-                            flipped[:, a * P : (a + 1) * P],
-                            tokens[c][:, a, kb * P : (kb + 1) * P],
-                            identity[:],
-                        )
-                    target = windows[kb][:, c * width : (c + 1) * width]
-                    if kb == 0:
-                        nc.vector.tensor_copy(target, flipped[:])
-                    else:
-                        nc.scalar.copy(target, flipped[:])
+        windows = [held.tile([P, S], BF16, name="window%d" % h) for h in range(HALVES)]
+        for c in range(LOADS):
+            flipped = flip.tile([P, TOKENS_A_LOAD], F32, name="flipped")
+            for a in range(NEIGHBOURS):
+                nc.tensor.transpose(flipped[:, a * P : (a + 1) * P], tokens[c][:, a, :].bitcast(F32), identity[:])
+            numbers = flipped[:].bitcast(BF16).rearrange("p (a q h) -> p h q a", a=NEIGHBOURS, h=HALVES)
+            columns = slice(c * TOKENS_A_LOAD, (c + 1) * TOKENS_A_LOAD)
+            nc.vector.tensor_copy(windows[0][:, columns].rearrange("p (q a) -> p q a", a=NEIGHBOURS), numbers[:, 0])
+            nc.scalar.copy(windows[1][:, columns].rearrange("p (q a) -> p q a", a=NEIGHBOURS), numbers[:, 1])
 
-        with tc.psum_pool(name="sums", bufs=PIECES * M_BLOCKS) as sums:
-            for piece in range(PIECES):
-                picked = offsets[:, piece * (PIECE // 16) : (piece + 1) * (PIECE // 16)]
+        for piece in range(PIECES):
+            picked = offsets[:, piece * (PIECE // 16) : (piece + 1) * (PIECE // 16)]
+            banks = [sums.tile([P, PIECE], F32, name="bank%d" % mb) for mb in range(M_BLOCKS)]
+            for h in range(HALVES):
                 for mb in range(M_BLOCKS):
-                    bank = sums.tile([P, PIECE], F32, name="bank")
-                    for kb in range(K_BLOCKS):
-                        nc.tensor.matmul(
-                            bank[:],
-                            weights[:, kb, mb * P : (mb + 1) * P],
-                            windows[kb][:].indirect(picked),
-                            start=(kb == 0),
-                            stop=(kb == K_BLOCKS - 1),
-                        )
-                    result = staging.tile([P, PIECE], F32, name="result")
-                    if mb == 0:
-                        nc.vector.tensor_scalar(result[:], bank[:], bias[:, mb : mb + 1], 0.0, op0=ADD, op1=MAX)
-                    else:
-                        nc.scalar.activation(result[:], bank[:], RELU, bias=bias[:, mb : mb + 1])
-                    nc.sync.dma_start(out[mb * P : (mb + 1) * P, piece * PIECE : (piece + 1) * PIECE], result[:])
+                    nc.tensor.matmul(
+                        banks[mb][:],
+                        weights[:, h, mb * P : (mb + 1) * P],
+                        windows[h][:].indirect(picked),
+                        start=(h == 0),
+                        stop=(h == HALVES - 1),
+                    )
+            for mb in range(M_BLOCKS):
+                result = staging.tile([P, PIECE], F32, name="result")
+                if mb == 0:
+                    nc.vector.tensor_scalar(result[:], banks[mb][:], bias[:, mb : mb + 1], 0.0, op0=ADD, op1=MAX)
+                else:
+                    nc.scalar.activation(result[:], banks[mb][:], RELU, bias=bias[:, mb : mb + 1])
+                nc.sync.dma_start(out[mb * P : (mb + 1) * P, piece * PIECE : (piece + 1) * PIECE], result[:])

@@ -39,9 +39,9 @@ def tile_gather_matmul_kernel(tc, table, w, b, offs, out):
         offsets = held.tile([P, N // 16], U16, name="offsets")
         nc.sync.dma_start(offsets[:], offs)
         weights = held.tile([P, HALVES, M], BF16, name="weights")
-        nc.scalar.dma_start(weights[:], w.rearrange("(p h) m -> p h m", h=HALVES))
+        nc.sync.dma_start(weights[:], w.rearrange("(p h) m -> p h m", h=HALVES))
         bias = held.tile([P, M_BLOCKS], F32, name="bias")
-        nc.scalar.dma_start(bias[:], b.rearrange("(mb p) o -> p (mb o)", p=P))
+        nc.sync.dma_start(bias[:], b.rearrange("(mb p) o -> p (mb o)", p=P))
 
         windows = [held.tile([P, S], BF16, name="window%d" % h) for h in range(HALVES)]
         for c in range(LOADS):

@@ -7,9 +7,8 @@ PIECE = 512
 HALVES = K // P
 M_BLOCKS = M // P
 PIECES = N // PIECE
-LOADS = 4
-TOKENS_A_LOAD = S // LOADS
-NEIGHBOURS = TOKENS_A_LOAD // P
+NEIGHBOURS = (4, 4, 4, 2, 2)
+FLIP_BANKS = 4
 
 FLOPS = 2 * K * M * N
 
@@ -23,18 +22,20 @@ def tile_gather_matmul_kernel(tc, table, w, b, offs, out):
     with (
         tc.tile_pool(name="held", bufs=1) as held,
         tc.tile_pool(name="staging", bufs=4) as staging,
-        tc.psum_pool(name="flip", bufs=LOADS) as flip,
+        tc.psum_pool(name="flip", bufs=FLIP_BANKS) as flip,
         tc.psum_pool(name="sums", bufs=2) as sums,
     ):
         identity = held.tile([P, P], F32, name="identity")
         make_identity(nc, identity[:])
 
-        table_rows = table.rearrange("(c p a) k -> c p a k", p=P, a=NEIGHBOURS)
-        tokens = []
-        for c in range(LOADS):
-            rows = held.tile([P, NEIGHBOURS, K], BF16, name="rows%d" % c)
-            nc.sync.dma_start(rows[:], table_rows[c])
-            tokens.append(rows)
+        loads = []
+        first = 0
+        for c, neighbours in enumerate(NEIGHBOURS):
+            count = P * neighbours
+            rows = held.tile([P, neighbours, K], BF16, name="rows%d" % c)
+            nc.sync.dma_start(rows[:], table[first : first + count, :].rearrange("(p a) k -> p a k", a=neighbours))
+            loads.append((slice(first, first + count), neighbours, rows))
+            first += count
 
         offsets = held.tile([P, N // 16], U16, name="offsets")
         nc.sync.dma_start(offsets[:], offs)
@@ -44,14 +45,13 @@ def tile_gather_matmul_kernel(tc, table, w, b, offs, out):
         nc.sync.dma_start(bias[:], b.rearrange("(mb p) o -> p (mb o)", p=P))
 
         windows = [held.tile([P, S], BF16, name="window%d" % h) for h in range(HALVES)]
-        for c in range(LOADS):
-            flipped = flip.tile([P, TOKENS_A_LOAD], F32, name="flipped")
-            for a in range(NEIGHBOURS):
-                nc.tensor.transpose(flipped[:, a * P : (a + 1) * P], tokens[c][:, a, :].bitcast(F32), identity[:])
-            numbers = flipped[:].bitcast(BF16).rearrange("p (a q h) -> p h q a", a=NEIGHBOURS, h=HALVES)
-            columns = slice(c * TOKENS_A_LOAD, (c + 1) * TOKENS_A_LOAD)
-            nc.vector.tensor_copy(windows[0][:, columns].rearrange("p (q a) -> p q a", a=NEIGHBOURS), numbers[:, 0])
-            nc.scalar.copy(windows[1][:, columns].rearrange("p (q a) -> p q a", a=NEIGHBOURS), numbers[:, 1])
+        for tokens, neighbours, rows in loads:
+            flipped = flip.tile([P, P * neighbours], F32, name="flipped")
+            for a in range(neighbours):
+                nc.tensor.transpose(flipped[:, a * P : (a + 1) * P], rows[:, a, :].bitcast(F32), identity[:])
+            numbers = flipped[:].bitcast(BF16).rearrange("p (a q h) -> p h q a", a=neighbours, h=HALVES)
+            nc.vector.tensor_copy(windows[0][:, tokens].rearrange("p (q a) -> p q a", a=neighbours), numbers[:, 0])
+            nc.scalar.copy(windows[1][:, tokens].rearrange("p (q a) -> p q a", a=neighbours), numbers[:, 1])
 
         for piece in range(PIECES):
             picked = offsets[:, piece * (PIECE // 16) : (piece + 1) * (PIECE // 16)]

@@ -56,8 +56,8 @@ def tile_gather_matmul_kernel(tc, table, w, b, offs, out):
         for piece in range(PIECES):
             picked = offsets[:, piece * (PIECE // 16) : (piece + 1) * (PIECE // 16)]
             banks = [sums.tile([P, PIECE], F32, name="bank%d" % mb) for mb in range(M_BLOCKS)]
-            for h in range(HALVES):
-                for mb in range(M_BLOCKS):
+            for mb in range(M_BLOCKS):
+                for h in range(HALVES):
                     nc.tensor.matmul(
                         banks[mb][:],
                         weights[:, h, mb * P : (mb + 1) * P],

@@ -67,7 +67,7 @@ def tile_gather_matmul_kernel(tc, table, w, b, offs, out):
                     )
             for mb in range(M_BLOCKS):
                 result = staging.tile([P, PIECE], F32, name="result")
-                if mb == 0:
+                if mb == M_BLOCKS - 1:
                     nc.vector.tensor_scalar(result[:], banks[mb][:], bias[:, mb : mb + 1], 0.0, op0=ADD, op1=MAX)
                 else:
                     nc.scalar.activation(result[:], banks[mb][:], RELU, bias=bias[:, mb : mb + 1])

@@ -45,13 +45,14 @@ def tile_gather_matmul_kernel(tc, table, w, b, offs, out):
         nc.sync.dma_start(bias[:], b.rearrange("(mb p) o -> p (mb o)", p=P))
 
         windows = [held.tile([P, S], BF16, name="window%d" % h) for h in range(HALVES)]
-        for tokens, neighbours, rows in loads:
+        for c, (tokens, neighbours, rows) in enumerate(loads):
             flipped = flip.tile([P, P * neighbours], F32, name="flipped")
             for a in range(neighbours):
                 nc.tensor.transpose(flipped[:, a * P : (a + 1) * P], rows[:, a, :].bitcast(F32), identity[:])
             numbers = flipped[:].bitcast(BF16).rearrange("p (a q h) -> p h q a", a=neighbours, h=HALVES)
             nc.vector.tensor_copy(windows[0][:, tokens].rearrange("p (q a) -> p q a", a=neighbours), numbers[:, 0])
-            nc.scalar.copy(windows[1][:, tokens].rearrange("p (q a) -> p q a", a=neighbours), numbers[:, 1])
+            copy_odd = nc.vector.tensor_copy if c == len(loads) - 1 else nc.scalar.copy
+            copy_odd(windows[1][:, tokens].rearrange("p (q a) -> p q a", a=neighbours), numbers[:, 1])
 
         for piece in range(PIECES):
             picked = offsets[:, piece * (PIECE // 16) : (piece + 1) * (PIECE // 16)]

@@ -7,8 +7,9 @@ PIECE = 512
 HALVES = K // P
 M_BLOCKS = M // P
 PIECES = N // PIECE
-NEIGHBOURS = (4, 4, 4, 2, 2)
-FLIP_BANKS = 4
+NEIGHBOURS = (2, 4, 4, 4, 2)
+FLIP_BANKS = 5
+WARM_UPS = 14
 
 FLOPS = 2 * K * M * N
 
@@ -23,10 +24,16 @@ def tile_gather_matmul_kernel(tc, table, w, b, offs, out):
         tc.tile_pool(name="held", bufs=1) as held,
         tc.tile_pool(name="staging", bufs=4) as staging,
         tc.psum_pool(name="flip", bufs=FLIP_BANKS) as flip,
-        tc.psum_pool(name="sums", bufs=2) as sums,
+        tc.psum_pool(name="sums", bufs=8 - FLIP_BANKS) as sums,
     ):
         identity = held.tile([P, P], F32, name="identity")
         make_identity(nc, identity[:])
+
+        zeros = held.tile([P, P], BF16, name="zeros")
+        nc.vector.memset(zeros[:], 0.0)
+        scrap = flip.tile([P, P], F32, name="scrap", tag="flipped")
+        for i in range(WARM_UPS):
+            nc.tensor.matmul(scrap[:], zeros[:], zeros[:], start=True, stop=True)
 
         loads = []
         first = 0
@@ -45,27 +52,32 @@ def tile_gather_matmul_kernel(tc, table, w, b, offs, out):
         nc.sync.dma_start(bias[:], b.rearrange("(mb p) o -> p (mb o)", p=P))
 
         windows = [held.tile([P, S], BF16, name="window%d" % h) for h in range(HALVES)]
-        for c, (tokens, neighbours, rows) in enumerate(loads):
+        numbers = []
+        for tokens, neighbours, rows in loads:
             flipped = flip.tile([P, P * neighbours], F32, name="flipped")
             for a in range(neighbours):
                 nc.tensor.transpose(flipped[:, a * P : (a + 1) * P], rows[:, a, :].bitcast(F32), identity[:])
-            numbers = flipped[:].bitcast(BF16).rearrange("p (a q h) -> p h q a", a=neighbours, h=HALVES)
-            nc.vector.tensor_copy(windows[0][:, tokens].rearrange("p (q a) -> p q a", a=neighbours), numbers[:, 0])
-            copy_odd = nc.vector.tensor_copy if c == len(loads) - 1 else nc.scalar.copy
-            copy_odd(windows[1][:, tokens].rearrange("p (q a) -> p q a", a=neighbours), numbers[:, 1])
+            numbers.append(flipped[:].bitcast(BF16).rearrange("p (a q h) -> p h q a", a=neighbours, h=HALVES))
+        copies = (nc.vector.tensor_copy, nc.scalar.copy)
+        for h in range(HALVES):
+            for c, (tokens, neighbours, rows) in enumerate(loads):
+                window = windows[h][:, tokens].rearrange("p (q a) -> p q a", a=neighbours)
+                copies[(c + h) % 2](window, numbers[c][:, h])
 
         for piece in range(PIECES):
             picked = offsets[:, piece * (PIECE // 16) : (piece + 1) * (PIECE // 16)]
-            banks = [sums.tile([P, PIECE], F32, name="bank%d" % mb) for mb in range(M_BLOCKS)]
-            for mb in range(M_BLOCKS):
-                for h in range(HALVES):
-                    nc.tensor.matmul(
-                        banks[mb][:],
-                        weights[:, h, mb * P : (mb + 1) * P],
-                        windows[h][:].indirect(picked),
-                        start=(h == 0),
-                        stop=(h == HALVES - 1),
-                    )
+            banks = [sums.tile([P, PIECE], F32, name="bank%d" % mb, tag="bank") for mb in range(M_BLOCKS)]
+            order = [(mb, h) for mb in range(M_BLOCKS) for h in range(HALVES)]
+            if piece == 0:
+                order = [(mb, h) for h in range(HALVES) for mb in range(M_BLOCKS)]
+            for mb, h in order:
+                nc.tensor.matmul(
+                    banks[mb][:],
+                    weights[:, h, mb * P : (mb + 1) * P],
+                    windows[h][:].indirect(picked),
+                    start=(h == 0),
+                    stop=(h == HALVES - 1),
+                )
             for mb in range(M_BLOCKS):
                 result = staging.tile([P, PIECE], F32, name="result")
                 if mb == M_BLOCKS - 1:

@@ -9,7 +9,7 @@ M_BLOCKS = M // P
 PIECES = N // PIECE
 NEIGHBOURS = (2, 4, 4, 4, 2)
 FLIP_BANKS = 5
-WARM_UPS = 14
+WARM_UPS = 2 * 1024 // P + 1
 
 FLOPS = 2 * K * M * N
 
@@ -22,7 +22,7 @@ def tile_gather_matmul_kernel(tc, table, w, b, offs, out):
     nc = tc.nc
     with (
         tc.tile_pool(name="held", bufs=1) as held,
-        tc.tile_pool(name="staging", bufs=4) as staging,
+        tc.tile_pool(name="staging", bufs=PIECES * M_BLOCKS) as staging,
         tc.psum_pool(name="flip", bufs=FLIP_BANKS) as flip,
         tc.psum_pool(name="sums", bufs=8 - FLIP_BANKS) as sums,
     ):

@@ -7,7 +7,7 @@ PIECE = 512
 HALVES = K // P
 M_BLOCKS = M // P
 PIECES = N // PIECE
-NEIGHBOURS = (2, 4, 4, 4, 2)
+NEIGHBOURS = (3, 4, 4, 4, 1)
 FLIP_BANKS = 5
 WARM_UPS = 2 * 1024 // P + 1
 

import concourse.mybir as mybir
from concourse.masks import make_identity

P = 128
S, K, M, N = 2048, 256, 256, 2048
PIECE = 512
HALVES = K // P
M_BLOCKS = M // P
PIECES = N // PIECE
NEIGHBOURS = (3, 4, 4, 4, 1)
FLIP_BANKS = 5
WARM_UPS = 2 * 1024 // P + 1

FLOPS = 2 * K * M * N

BF16, F32, U16 = mybir.dt.bfloat16, mybir.dt.float32, mybir.dt.uint16
ADD, MAX = mybir.AluOpType.add, mybir.AluOpType.max
RELU = mybir.ActivationFunctionType.Relu


def tile_gather_matmul_kernel(tc, table, w, b, offs, out):
    nc = tc.nc
    with (
        tc.tile_pool(name="held", bufs=1) as held,
        tc.tile_pool(name="staging", bufs=PIECES * M_BLOCKS) as staging,
        tc.psum_pool(name="flip", bufs=FLIP_BANKS) as flip,
        tc.psum_pool(name="sums", bufs=8 - FLIP_BANKS) as sums,
    ):
        identity = held.tile([P, P], F32, name="identity")
        make_identity(nc, identity[:])

        zeros = held.tile([P, P], BF16, name="zeros")
        nc.vector.memset(zeros[:], 0.0)
        scrap = flip.tile([P, P], F32, name="scrap", tag="flipped")
        for i in range(WARM_UPS):
            nc.tensor.matmul(scrap[:], zeros[:], zeros[:], start=True, stop=True)

        loads = []
        first = 0
        for c, neighbours in enumerate(NEIGHBOURS):
            count = P * neighbours
            rows = held.tile([P, neighbours, K], BF16, name="rows%d" % c)
            nc.sync.dma_start(rows[:], table[first : first + count, :].rearrange("(p a) k -> p a k", a=neighbours))
            loads.append((slice(first, first + count), neighbours, rows))
            first += count

        offsets = held.tile([P, N // 16], U16, name="offsets")
        nc.sync.dma_start(offsets[:], offs)
        weights = held.tile([P, HALVES, M], BF16, name="weights")
        nc.sync.dma_start(weights[:], w.rearrange("(p h) m -> p h m", h=HALVES))
        bias = held.tile([P, M_BLOCKS], F32, name="bias")
        nc.sync.dma_start(bias[:], b.rearrange("(mb p) o -> p (mb o)", p=P))

        windows = [held.tile([P, S], BF16, name="window%d" % h) for h in range(HALVES)]
        numbers = []
        for tokens, neighbours, rows in loads:
            flipped = flip.tile([P, P * neighbours], F32, name="flipped")
            for a in range(neighbours):
                nc.tensor.transpose(flipped[:, a * P : (a + 1) * P], rows[:, a, :].bitcast(F32), identity[:])
            numbers.append(flipped[:].bitcast(BF16).rearrange("p (a q h) -> p h q a", a=neighbours, h=HALVES))
        copies = (nc.vector.tensor_copy, nc.scalar.copy)
        for h in range(HALVES):
            for c, (tokens, neighbours, rows) in enumerate(loads):
                window = windows[h][:, tokens].rearrange("p (q a) -> p q a", a=neighbours)
                copies[(c + h) % 2](window, numbers[c][:, h])

        for piece in range(PIECES):
            picked = offsets[:, piece * (PIECE // 16) : (piece + 1) * (PIECE // 16)]
            banks = [sums.tile([P, PIECE], F32, name="bank%d" % mb, tag="bank") for mb in range(M_BLOCKS)]
            order = [(mb, h) for mb in range(M_BLOCKS) for h in range(HALVES)]
            if piece == 0:
                order = [(mb, h) for h in range(HALVES) for mb in range(M_BLOCKS)]
            for mb, h in order:
                nc.tensor.matmul(
                    banks[mb][:],
                    weights[:, h, mb * P : (mb + 1) * P],
                    windows[h][:].indirect(picked),
                    start=(h == 0),
                    stop=(h == HALVES - 1),
                )
            for mb in range(M_BLOCKS):
                result = staging.tile([P, PIECE], F32, name="result")
                if mb == M_BLOCKS - 1:
                    nc.vector.tensor_scalar(result[:], banks[mb][:], bias[:, mb : mb + 1], 0.0, op0=ADD, op1=MAX)
                else:
                    nc.scalar.activation(result[:], banks[mb][:], RELU, bias=bias[:, mb : mb + 1])
                nc.sync.dma_start(out[mb * P : (mb + 1) * P, piece * PIECE : (piece + 1) * PIECE], result[:])
